import numpy as np
import ml_dtypes


def mxq(x, axis, fmt="e4m3"):
    dtype, down = {"e4m3": (ml_dtypes.float8_e4m3fn, 7), "e5m2": (ml_dtypes.float8_e5m2, 14)}[fmt]
    v = np.moveaxis(np.asarray(x, np.float32).astype(ml_dtypes.bfloat16).astype(np.float64), axis, -1)
    blocks = v.reshape(v.shape[:-1] + (-1, 32))
    amax = np.abs(blocks).max(-1, keepdims=True)
    byte = np.maximum(np.where(amax > 0, np.frexp(amax)[1] - 1 + 127, 0) - down, 1)
    scale = np.exp2(byte - 127.0)
    codes = (blocks / scale).astype(np.float32).astype(dtype).astype(np.float64)
    return np.moveaxis((codes * scale).reshape(v.shape), -1, axis)


WIDE = False


def mx_kscale(k):
    if not WIDE:
        return np.ones(k)
    levels = np.array([10, -10, 5, -5, 0])
    if k % 512:
        return np.exp2(np.random.permutation(np.resize(levels, k // 32))).repeat(32)
    a = np.empty((k // 512, 16))
    for p in range(k // 512):
        a[p, :8] = np.random.permutation(np.resize(levels, 8))
        for g in range(8):
            far = levels[np.abs(levels - a[p, g]) >= 10]
            a[p, g + 8] = far[np.random.randint(len(far))]
    return np.exp2(a.ravel()).repeat(32)


def f64(x):
    return np.asarray(x).astype(np.float64)


def striped(idx):
    return np.tile(idx.reshape(-1, 16).T, (8, 1)).astype(np.uint16)


def unstriped(offs):
    return offs[:16].T.reshape(-1).astype(np.int64)


E2M1 = np.array([0.0, 0.5, 1.0, 1.5, 2.0, 3.0, 4.0, 6.0, -0.0, -0.5, -1.0, -1.5, -2.0, -3.0, -4.0, -6.0])


def pack_weight(w, fmt):
    k, n = w.shape
    w = f64(np.asarray(w, np.float32).astype(ml_dtypes.bfloat16)).reshape(k // 32, 32, n)
    amax = np.abs(w).max(1)
    if fmt == "e4m3":
        byte = np.frexp(amax)[1] - 1 + 127 - 7
    else:
        mant, ex = np.frexp(amax / 6.0)
        byte = np.where(mant > 0.5, ex, ex - 1) + 127
    byte = np.clip(np.where(amax > 0, byte, 1), 1, 254)
    scaled = (w * np.exp2(127.0 - byte)[:, None, :]).reshape(k, n).astype(np.float32)
    by_word = np.ascontiguousarray(scaled.reshape(k // 512, 128, 4, n).transpose(0, 1, 3, 2))
    if fmt == "e4m3":
        words = by_word.astype(ml_dtypes.float8_e4m3fn).view(np.uint8)
    else:
        c = by_word.astype(ml_dtypes.float4_e2m1fn).view(np.uint8) & 0xF
        words = (c[..., 0::2] | (c[..., 1::2] << 4)).reshape(k // 512, 128, 2 * n)
    return np.ascontiguousarray(words), np.ascontiguousarray(byte.astype(np.uint8).reshape(k // 512, 16, n))


def unpack_weight(words, scales, fmt):
    g, _, n = scales.shape
    words = np.ascontiguousarray(words).reshape(g, 128, n, -1)
    if fmt == "e4m3":
        vals = words.view(ml_dtypes.float8_e4m3fn).astype(np.float64)
    else:
        nib = np.empty((g, 128, n, 4), np.uint8)
        nib[..., 0::2] = words & 0xF
        nib[..., 1::2] = words >> 4
        vals = E2M1[nib]
    vals = vals * np.repeat(np.exp2(scales.astype(np.float64) - 127.0), 8, axis=1)[..., None]
    return vals.transpose(0, 1, 3, 2).reshape(g * 512, n)


def relu(v):
    return np.maximum(v, 0.0)


K, T, E, C, H, N = 1024, 1024, 8, 128, 512, 128
TOP = 3
PAD = 64


def by_expert(wq, xq):
    return np.concatenate([wq[e].T @ xq[:, e * C:(e + 1) * C] for e in range(E)], axis=1)


def setup_inputs():
    n = np.random.standard_normal
    s = mx_kscale(K)[:, None]
    u = mx_kscale(H)
    slot_token = np.empty(E * C, np.int64); pos = np.tile(E * C + np.arange(T) % PAD, (TOP, 1)); taken = np.zeros(T, np.int64)
    liked = np.random.randn(T)
    for e in np.random.permutation(E):
        free = np.flatnonzero(taken < TOP); pick = np.random.permutation(free[np.argsort(-(liked[free] + np.random.gumbel(size=free.size)))[:C]]); slot_token[e * C:(e + 1) * C] = pick
        pos[taken[pick], pick] = e * C + np.arange(C); taken[pick] += 1
    g = np.random.uniform(0.2, 0.8, (TOP, T))
    x = pack_weight(n((K, T)) * s, "e4m3")
    return {
        "x_words": x[0],
        "x_scales": x[1],
        "w1": (n((E, K, H)) / np.sqrt(K) / s[None]).astype(np.float32),
        "w3": (n((E, K, H)) / np.sqrt(K) / s[None] * u[None, None, :]).astype(np.float32),
        "w2": (n((E, H, N)) / np.sqrt(H) / u[None, :, None]).astype(np.float32),
        "gate": np.stack([np.tile(r, (N, 1)) for r in g]).astype(np.float32),
        "offs": striped(slot_token),
        "pos1": striped(pos[0]),
        "pos2": striped(pos[1]),
        "pos3": striped(pos[2]),
    }


def reference(x_words, x_scales, w1, w3, w2, gate, offs, pos1, pos2, pos3):
    idx = unstriped(offs)
    xq = unpack_weight(x_words, x_scales, "e4m3")[:, idx]
    h = relu(by_expert(mxq(f64(w1), 1, "e4m3"), xq))
    h = h * by_expert(mxq(f64(w3), 1, "e4m3"), xq)
    y = by_expert(mxq(f64(w2), 1, "e4m3"), mxq(h, 0, "e4m3"))
    y = np.concatenate([y, np.zeros((N, PAD))], axis=1)
    return sum(f64(gate[r]) * y[:, unstriped(p)] for r, p in enumerate((pos1, pos2, pos3)))

@@ -1,0 +1,183 @@
+from contextlib import ExitStack
+
+import concourse.mybir as mybir
+
+K, T, E, C, H, N = 1024, 1024, 8, 128, 512, 128
+TOP = 3
+PAD = 64
+FLOPS = 2 * E * C * (2 * K * H + H * N)
+
+F32 = mybir.dt.float32
+BF16 = mybir.dt.bfloat16
+I32 = mybir.dt.int32
+U32 = mybir.dt.uint32
+U16 = mybir.dt.uint16
+U8 = mybir.dt.uint8
+FP8X4 = mybir.dt.float8_e4m3fn_x4
+MULT = mybir.AluOpType.mult
+ADD = mybir.AluOpType.add
+RELU = mybir.ActivationFunctionType.Relu
+
+P = 128
+PACK = 4
+K_PASS = P * PACK
+PASSES = K // K_PASS
+SLOTS = E * C
+PER_COL = 16
+GATHER = 256
+CHUNKS = (512, 384, 128)
+
+
+def tile_moe_ecr_glu_relu_kernel(
+    tc, x_words, x_scales, w1, w3, w2, gate, offs, pos1, pos2, pos3, out
+):
+    nc = tc.nc
+    with ExitStack() as ctx:
+        keep = ctx.enter_context(tc.tile_pool(name="keep", bufs=1))
+        stream = ctx.enter_context(tc.tile_pool(name="stream", bufs=12))
+        rounded = ctx.enter_context(tc.tile_pool(name="rounded", bufs=6))
+        coded = ctx.enter_context(tc.tile_pool(name="coded", bufs=12))
+        small = ctx.enter_context(tc.tile_pool(name="small", bufs=3))
+        psum = ctx.enter_context(tc.psum_pool(name="psum", bufs=2))
+
+        def load_rows(rows):
+            raw = stream.tile([P, PACK, rows.shape[1]], F32, name="raw")
+            nc.sync.dma_start(out=raw[:], in_=rows.rearrange("(p j) c -> p j c", j=PACK))
+            return raw
+
+        def quantize(values, pool, name):
+            width = values.shape[1] // PACK
+            codes = pool.tile([P, width], U32, name=name + "_codes", align_bytes=64)
+            scales = pool.tile([P, width], U8, name=name + "_scales", align_bytes=64)
+            nc.vector.quantize_mx(out=codes[:].bitcast(FP8X4), scales=scales[:], in_=values)
+            return codes, scales
+
+        def quantize_first_layer(raw):
+            src = raw[:].rearrange("p j (m t) -> p m t j", t=PACK)
+            halves = []
+            for u, copy in enumerate((nc.vector.tensor_copy, nc.scalar.copy)):
+                half = rounded.tile([P, 2 * P * PACK], BF16, name="half", align_bytes=64)
+                copy(
+                    out=half[:].rearrange("p (t m j) -> p m t j", t=2, j=PACK),
+                    in_=src[:, :, 2 * u : 2 * u + 2, :],
+                )
+                halves.append(half)
+            return [quantize(half[:], coded, "w") for half in halves]
+
+        first = load_rows(w1[0, 0:K_PASS, :])
+
+        offs_sb = keep.tile([P, SLOTS // PER_COL], U16, name="offs_sb")
+        nc.sync.dma_start(offs_sb[:], offs)
+        xs = keep.tile([P, T], U8, name="xs", align_bytes=64)
+        nc.vector.memset(xs[:].bitcast(I32), 0)
+        for q in range(4):
+            nc.scalar.dma_start(
+                out=xs[32 * q : 32 * q + 4 * PASSES, :].bitcast(I32),
+                in_=x_scales[:, 4 * q : 4 * q + 4, :].bitcast(I32),
+            )
+        xw = []
+        for o in range(PASSES):
+            words = keep.tile([P, T], I32, name="xw%d" % o, align_bytes=64)
+            nc.sync.dma_start(out=words[:], in_=x_words[o].rearrange("p t r -> p (t r)").bitcast(I32))
+            xw.append(words)
+
+        y_all = keep.tile([P, SLOTS + PAD], F32, name="y_all")
+        nc.vector.memset(y_all[:, SLOTS:], 0.0)
+
+        def gather_tokens(g):
+            idx = offs_sb[:, g * GATHER // PER_COL : (g + 1) * GATHER // PER_COL]
+            words = []
+            for o in range(PASSES):
+                gw = keep.tile([P, GATHER], U32, name="gw%d_%d" % (g, o), align_bytes=64)
+                nc.vector.tensor_copy(gw[:], xw[o][:].bitcast(U32).indirect(idx))
+                words.append(gw)
+            gs = keep.tile([P, GATHER], U8, name="gs%d" % g, align_bytes=64)
+            nc.vector.tensor_copy(gs[:], xs[:].indirect(idx))
+            return words, gs
+
+        def first_layer(acc, passes, tokens, cols):
+            words, gs = tokens
+            for t in range(PACK):
+                mcols = slice((t % 2) * P, (t % 2 + 1) * P)
+                for o in range(PASSES):
+                    codes, scales = passes[o][t // 2]
+                    nc.tensor.matmul_mx(
+                        out=acc[:, t, :],
+                        lhsT=codes[:, mcols].bitcast(FP8X4),
+                        lhsT_scale=scales[:, mcols],
+                        rhs=words[o][:, cols].bitcast(FP8X4),
+                        rhs_scale=gs[4 * o : P, cols],
+                        start=(o == 0),
+                        stop=(o == PASSES - 1),
+                    )
+
+        tokens = None
+        for e in range(E):
+            cols = slice(e * C % GATHER, e * C % GATHER + C)
+            passes = []
+            for o in range(PASSES):
+                raw = first if (e, o) == (0, 0) else load_rows(w1[e, o * K_PASS : (o + 1) * K_PASS, :])
+                passes.append(quantize_first_layer(raw))
+            if e * C % GATHER == 0:
+                tokens = gather_tokens(e * C // GATHER)
+            a_ps = psum.tile([P, PACK, C], F32, name="a_ps")
+            first_layer(a_ps, passes, tokens, cols)
+            relu_a = small.tile([P, C, PACK], F32, name="relu_a")
+            nc.scalar.activation(relu_a[:], a_ps[:].rearrange("p t c -> p c t"), RELU)
+
+            passes = [quantize_first_layer(load_rows(w3[e, o * K_PASS : (o + 1) * K_PASS, :])) for o in range(PASSES)]
+            b_ps = psum.tile([P, PACK, C], F32, name="b_ps")
+            first_layer(b_ps, passes, tokens, cols)
+
+            raw2 = load_rows(w2[e])
+            w2_bf = small.tile([P, N, PACK], BF16, name="w2_bf", align_bytes=64)
+            nc.scalar.copy(out=w2_bf[:], in_=raw2[:].rearrange("p j n -> p n j"))
+
+            h_bf = small.tile([P, C, PACK], BF16, name="h_bf", align_bytes=64)
+            nc.vector.tensor_tensor(h_bf[:], b_ps[:].rearrange("p t c -> p c t"), relu_a[:], MULT)
+            w2_codes, w2_scales = quantize(w2_bf[:].rearrange("p n j -> p (n j)"), small, "w2")
+            h_codes, h_scales = quantize(h_bf[:].rearrange("p c t -> p (c t)"), small, "h")
+            y_ps = psum.tile([P, C], F32, name="y_ps")
+            nc.tensor.matmul_mx(
+                out=y_ps[:],
+                lhsT=w2_codes[:].bitcast(FP8X4),
+                lhsT_scale=w2_scales[:],
+                rhs=h_codes[:].bitcast(FP8X4),
+                rhs_scale=h_scales[:],
+                start=True,
+                stop=True,
+            )
+            nc.scalar.copy(out=y_all[:, e * C : (e + 1) * C], in_=y_ps[:])
+
+        lists, gates = [], []
+        for r, pos in enumerate((pos1, pos2, pos3)):
+            pos_sb = keep.tile([P, T // PER_COL], U16, name="pos%d" % r)
+            nc.sync.dma_start(pos_sb[:], pos)
+            lists.append(pos_sb)
+            gate_sb = stream.tile([P, T], F32, name="raw")
+            nc.sync.dma_start(out=gate_sb[:], in_=gate[r])
+            gates.append(gate_sb)
+
+        t0 = 0
+        pending = None
+        for i, width in enumerate(CHUNKS):
+            cols = slice(t0, t0 + width)
+            parts = []
+            for r in range(TOP):
+                part = keep.tile([P, width], F32, name="part%d_%d" % (i, r))
+                idx = lists[r][:, t0 // PER_COL : (t0 + width) // PER_COL]
+                nc.vector.tensor_tensor(part[:], y_all[:].indirect(idx), gates[r][:, cols], MULT)
+                parts.append(part)
+                if r == 0 and pending is not None:
+                    pending()
+            two = keep.tile([P, width], F32, name="two%d" % i)
+            nc.vector.tensor_tensor(two[:], parts[0][:], parts[1][:], ADD)
+
+            def finish(two=two, third=parts[2], cols=cols, width=width, i=i):
+                total = keep.tile([P, width], F32, name="total%d" % i)
+                nc.vector.tensor_tensor(total[:], two[:], third[:], ADD)
+                nc.sync.dma_start(out=out[:, cols], in_=total[:])
+
+            pending = finish
+            t0 += width
+        pending()

@@ -25,6 +25,7 @@ PASSES = K // K_PASS
 SLOTS = E * C
 PER_COL = 16
 GATHER = 256
+Y_GROUPS = ((0, 4), (4, 7), (7, 8))
 CHUNKS = (512, 384, 128)
 
 
@@ -35,8 +36,8 @@ def tile_moe_ecr_glu_relu_kernel(
     with ExitStack() as ctx:
         keep = ctx.enter_context(tc.tile_pool(name="keep", bufs=1))
         stream = ctx.enter_context(tc.tile_pool(name="stream", bufs=12))
-        rounded = ctx.enter_context(tc.tile_pool(name="rounded", bufs=6))
-        coded = ctx.enter_context(tc.tile_pool(name="coded", bufs=12))
+        rounded = ctx.enter_context(tc.tile_pool(name="rounded", bufs=1))
+        coded = ctx.enter_context(tc.tile_pool(name="coded", bufs=4))
         small = ctx.enter_context(tc.tile_pool(name="small", bufs=3))
         psum = ctx.enter_context(tc.psum_pool(name="psum", bufs=2))
 
@@ -52,17 +53,24 @@ def tile_moe_ecr_glu_relu_kernel(
             nc.vector.quantize_mx(out=codes[:].bitcast(FP8X4), scales=scales[:], in_=values)
             return codes, scales
 
-        def quantize_first_layer(raw):
-            src = raw[:].rearrange("p j (m t) -> p m t j", t=PACK)
+        def quantize_first_layer(raw, place, between=None):
+            src = raw[:].rearrange("p j (m t) -> p m j t", t=PACK)
+            codes = coded.tile([P, H], U32, name="w_codes", align_bytes=64)
+            scales = coded.tile([P, H], U8, name="w_scales", align_bytes=64)
             halves = []
             for u, copy in enumerate((nc.vector.tensor_copy, nc.scalar.copy)):
-                half = rounded.tile([P, 2 * P * PACK], BF16, name="half", align_bytes=64)
+                half = rounded.tile([P, 2 * H], BF16, name="half%d_%d" % (place, u), align_bytes=64)
                 copy(
-                    out=half[:].rearrange("p (t m j) -> p m t j", t=2, j=PACK),
-                    in_=src[:, :, 2 * u : 2 * u + 2, :],
+                    out=half[:].rearrange("p (t m j) -> p m j t", t=2, j=PACK),
+                    in_=src[:, :, :, 2 * u : 2 * u + 2],
                 )
                 halves.append(half)
-            return [quantize(half[:], coded, "w") for half in halves]
+            for u in range(2):
+                cols = slice(u * H // 2, (u + 1) * H // 2)
+                nc.vector.quantize_mx(out=codes[:, cols].bitcast(FP8X4), scales=scales[:, cols], in_=halves[u][:])
+                if between is not None:
+                    between[u]()
+            return codes, scales
 
         first = load_rows(w1[0, 0:K_PASS, :])
 
@@ -98,9 +106,9 @@ def tile_moe_ecr_glu_relu_kernel(
         def first_layer(acc, passes, tokens, cols):
             words, gs = tokens
             for t in range(PACK):
-                mcols = slice((t % 2) * P, (t % 2 + 1) * P)
+                mcols = slice(t * P, (t + 1) * P)
                 for o in range(PASSES):
-                    codes, scales = passes[o][t // 2]
+                    codes, scales = passes[o]
                     nc.tensor.matmul_mx(
                         out=acc[:, t, :],
                         lhsT=codes[:, mcols].bitcast(FP8X4),
@@ -111,43 +119,66 @@ def tile_moe_ecr_glu_relu_kernel(
                         stop=(o == PASSES - 1),
                     )
 
+        y_banks = {}
+
+        def second_layer(e, b_ps, relu_a, w2_q):
+            held = {}
+
+            def gate_hidden():
+                name = "half0_0" if e < E - 1 else "h_last"
+                h_bf = rounded.tile([P, C, PACK], BF16, name=name, align_bytes=64)
+                nc.vector.tensor_tensor(h_bf[:], b_ps[:].rearrange("p t c -> p c t"), relu_a[:], MULT)
+                held["h"] = h_bf
+
+            def multiply():
+                h_codes, h_scales = quantize(held["h"][:].rearrange("p c t -> p (c t)"), small, "h")
+                lo, hi = [g for g in Y_GROUPS if g[0] <= e < g[1]][0]
+                if e == lo:
+                    y_banks[lo] = psum.tile([P, (hi - lo) * C], F32, name="y_ps")
+                y_ps = y_banks[lo]
+                nc.tensor.matmul_mx(
+                    out=y_ps[:, (e - lo) * C : (e - lo + 1) * C],
+                    lhsT=w2_q[0][:].bitcast(FP8X4),
+                    lhsT_scale=w2_q[1][:],
+                    rhs=h_codes[:].bitcast(FP8X4),
+                    rhs_scale=h_scales[:],
+                    start=True,
+                    stop=True,
+                )
+                if e == hi - 1:
+                    nc.scalar.copy(out=y_all[:, lo * C : hi * C], in_=y_ps[:])
+
+            return gate_hidden, multiply
+
         tokens = None
+        behind = None
         for e in range(E):
             cols = slice(e * C % GATHER, e * C % GATHER + C)
-            passes = []
-            for o in range(PASSES):
-                raw = first if (e, o) == (0, 0) else load_rows(w1[e, o * K_PASS : (o + 1) * K_PASS, :])
-                passes.append(quantize_first_layer(raw))
+            raw = first if e == 0 else load_rows(w1[e, 0:K_PASS, :])
+            w1_q = [quantize_first_layer(raw, 0, behind)]
+            w1_q.append(quantize_first_layer(load_rows(w1[e, K_PASS:K, :]), 1))
             if e * C % GATHER == 0:
                 tokens = gather_tokens(e * C // GATHER)
             a_ps = psum.tile([P, PACK, C], F32, name="a_ps")
-            first_layer(a_ps, passes, tokens, cols)
-            relu_a = small.tile([P, C, PACK], F32, name="relu_a")
-            nc.scalar.activation(relu_a[:], a_ps[:].rearrange("p t c -> p c t"), RELU)
+            first_layer(a_ps, w1_q, tokens, cols)
 
-            passes = [quantize_first_layer(load_rows(w3[e, o * K_PASS : (o + 1) * K_PASS, :])) for o in range(PASSES)]
+            w3_q = [quantize_first_layer(load_rows(w3[e, 0:K_PASS, :]), 2)]
+            relu_a = rounded.tile([P, C, PACK], F32, name="half2_0", align_bytes=64)
+            nc.scalar.activation(relu_a[:], a_ps[:].rearrange("p t c -> p c t"), RELU)
+            w3_q.append(quantize_first_layer(load_rows(w3[e, K_PASS:K, :]), 3))
             b_ps = psum.tile([P, PACK, C], F32, name="b_ps")
-            first_layer(b_ps, passes, tokens, cols)
+            first_layer(b_ps, w3_q, tokens, cols)
 
             raw2 = load_rows(w2[e])
             w2_bf = small.tile([P, N, PACK], BF16, name="w2_bf", align_bytes=64)
-            nc.scalar.copy(out=w2_bf[:], in_=raw2[:].rearrange("p j n -> p n j"))
-
-            h_bf = small.tile([P, C, PACK], BF16, name="h_bf", align_bytes=64)
-            nc.vector.tensor_tensor(h_bf[:], b_ps[:].rearrange("p t c -> p c t"), relu_a[:], MULT)
-            w2_codes, w2_scales = quantize(w2_bf[:].rearrange("p n j -> p (n j)"), small, "w2")
-            h_codes, h_scales = quantize(h_bf[:].rearrange("p c t -> p (c t)"), small, "h")
-            y_ps = psum.tile([P, C], F32, name="y_ps")
-            nc.tensor.matmul_mx(
-                out=y_ps[:],
-                lhsT=w2_codes[:].bitcast(FP8X4),
-                lhsT_scale=w2_scales[:],
-                rhs=h_codes[:].bitcast(FP8X4),
-                rhs_scale=h_scales[:],
-                start=True,
-                stop=True,
+            nc.scalar.copy(
+                out=w2_bf[:].rearrange("p (c i) j -> p c j i", i=4),
+                in_=raw2[:].rearrange("p j (c i) -> p c j i", i=4),
             )
-            nc.scalar.copy(out=y_all[:, e * C : (e + 1) * C], in_=y_ps[:])
+            w2_q = quantize(w2_bf[:].rearrange("p n j -> p (n j)"), small, "w2")
+            behind = second_layer(e, b_ps, relu_a, w2_q)
+        for step in behind:
+            step()
 
         lists, gates = [], []
         for r, pos in enumerate((pos1, pos2, pos3)):

@@ -1,6 +1,7 @@
 from contextlib import ExitStack
 
 import concourse.mybir as mybir
+from concourse.masks import make_identity
 
 K, T, E, C, H, N = 1024, 1024, 8, 128, 512, 128
 TOP = 3
@@ -25,8 +26,13 @@ PASSES = K // K_PASS
 SLOTS = E * C
 PER_COL = 16
 GATHER = 256
-Y_GROUPS = ((0, 4), (4, 7), (7, 8))
-CHUNKS = (512, 384, 128)
+Y_GROUPS = ((0, 4), (4, 6), (6, 7), (7, 8))
+W2_GROUP = 2
+W2_AFTER = (0, 2, 4, 7)
+WHOLE = 2 * E - 3
+LAST_SHARE = 32
+CHUNKS = (256, 256, 256, 128, 128)
+ON_TENSOR = 3
 
 
 def tile_moe_ecr_glu_relu_kernel(
@@ -35,44 +41,50 @@ def tile_moe_ecr_glu_relu_kernel(
     nc = tc.nc
     with ExitStack() as ctx:
         keep = ctx.enter_context(tc.tile_pool(name="keep", bufs=1))
-        stream = ctx.enter_context(tc.tile_pool(name="stream", bufs=12))
+        stream = ctx.enter_context(tc.tile_pool(name="stream", bufs=8))
         rounded = ctx.enter_context(tc.tile_pool(name="rounded", bufs=1))
         coded = ctx.enter_context(tc.tile_pool(name="coded", bufs=4))
-        small = ctx.enter_context(tc.tile_pool(name="small", bufs=3))
-        psum = ctx.enter_context(tc.psum_pool(name="psum", bufs=2))
+        small = ctx.enter_context(tc.tile_pool(name="small", bufs=4))
+        psum = ctx.enter_context(tc.psum_pool(name="psum", bufs=1))
 
-        def load_rows(rows):
-            raw = stream.tile([P, PACK, rows.shape[1]], F32, name="raw")
-            nc.sync.dma_start(out=raw[:], in_=rows.rearrange("(p j) c -> p j c", j=PACK))
+        def load_blocks(rows):
+            blocks = rows.shape[0] // K_PASS
+            raw = stream.tile([P, blocks, PACK, rows.shape[1]], F32, name="raw")
+            nc.sync.dma_start(out=raw[:], in_=rows.rearrange("(g p j) c -> p g j c", p=P, j=PACK))
             return raw
 
-        def quantize(values, pool, name):
+        def quantize(values, name, codes=None):
             width = values.shape[1] // PACK
-            codes = pool.tile([P, width], U32, name=name + "_codes", align_bytes=64)
-            scales = pool.tile([P, width], U8, name=name + "_scales", align_bytes=64)
+            if codes is None:
+                codes = small.tile([P, width], U32, name=name + "_codes", align_bytes=64)
+            scales = small.tile([P, width], U8, name=name + "_scales", align_bytes=64)
             nc.vector.quantize_mx(out=codes[:].bitcast(FP8X4), scales=scales[:], in_=values)
             return codes, scales
 
-        def quantize_first_layer(raw, place, between=None):
-            src = raw[:].rearrange("p j (m t) -> p m j t", t=PACK)
+        def round_pass(raw, place, vector_extra=0):
+            src = raw.rearrange("p j (m t) -> p m j t", t=PACK)
+            halves, views = [], []
+            for u in range(2):
+                half = rounded.tile([P, 2 * H], BF16, name="half%d_%d" % (place, u), align_bytes=64)
+                halves.append(half)
+                views.append(half[:].rearrange("p (t m j) -> p m j t", t=2, j=PACK))
+            nc.vector.tensor_copy(out=views[0], in_=src[:, :, :, 0:2])
+            if vector_extra:
+                nc.vector.tensor_copy(out=views[1][:, 0:vector_extra], in_=src[:, 0:vector_extra, :, 2:4])
+            nc.scalar.copy(out=views[1][:, vector_extra:P], in_=src[:, vector_extra:P, :, 2:4])
+            return halves
+
+        def quantize_pass(halves, between=None):
             codes = coded.tile([P, H], U32, name="w_codes", align_bytes=64)
             scales = coded.tile([P, H], U8, name="w_scales", align_bytes=64)
-            halves = []
-            for u, copy in enumerate((nc.vector.tensor_copy, nc.scalar.copy)):
-                half = rounded.tile([P, 2 * H], BF16, name="half%d_%d" % (place, u), align_bytes=64)
-                copy(
-                    out=half[:].rearrange("p (t m j) -> p m j t", t=2, j=PACK),
-                    in_=src[:, :, :, 2 * u : 2 * u + 2],
-                )
-                halves.append(half)
             for u in range(2):
                 cols = slice(u * H // 2, (u + 1) * H // 2)
                 nc.vector.quantize_mx(out=codes[:, cols].bitcast(FP8X4), scales=scales[:, cols], in_=halves[u][:])
-                if between is not None:
-                    between[u]()
+                if between is not None and u == 0:
+                    between()
             return codes, scales
 
-        first = load_rows(w1[0, 0:K_PASS, :])
+        first = load_blocks(w1[0])
 
         offs_sb = keep.tile([P, SLOTS // PER_COL], U16, name="offs_sb")
         nc.sync.dma_start(offs_sb[:], offs)
@@ -83,21 +95,20 @@ def tile_moe_ecr_glu_relu_kernel(
                 out=xs[32 * q : 32 * q + 4 * PASSES, :].bitcast(I32),
                 in_=x_scales[:, 4 * q : 4 * q + 4, :].bitcast(I32),
             )
-        xw = []
-        for o in range(PASSES):
-            words = keep.tile([P, T], I32, name="xw%d" % o, align_bytes=64)
-            nc.sync.dma_start(out=words[:], in_=x_words[o].rearrange("p t r -> p (t r)").bitcast(I32))
-            xw.append(words)
+        xw = keep.tile([P, PASSES, T], I32, name="xw", align_bytes=64)
+        nc.sync.dma_start(out=xw[:], in_=x_words.rearrange("o p t r -> p o (t r)").bitcast(I32))
 
         y_all = keep.tile([P, SLOTS + PAD], F32, name="y_all")
         nc.vector.memset(y_all[:, SLOTS:], 0.0)
+        ident = keep.tile([P, P], F32, name="ident")
+        make_identity(nc, ident[:])
 
         def gather_tokens(g):
             idx = offs_sb[:, g * GATHER // PER_COL : (g + 1) * GATHER // PER_COL]
             words = []
             for o in range(PASSES):
                 gw = keep.tile([P, GATHER], U32, name="gw%d_%d" % (g, o), align_bytes=64)
-                nc.vector.tensor_copy(gw[:], xw[o][:].bitcast(U32).indirect(idx))
+                nc.vector.tensor_copy(gw[:], xw[:, o, :].bitcast(U32).indirect(idx))
                 words.append(gw)
             gs = keep.tile([P, GATHER], U8, name="gs%d" % g, align_bytes=64)
             nc.vector.tensor_copy(gs[:], xs[:].indirect(idx))
@@ -119,9 +130,26 @@ def tile_moe_ecr_glu_relu_kernel(
                         stop=(o == PASSES - 1),
                     )
 
-        y_banks = {}
+        y_banks, w2_q, h_q = {}, {}, {}
 
-        def second_layer(e, b_ps, relu_a, w2_q):
+        def second_layer(e):
+            lo, hi = [g for g in Y_GROUPS if g[0] <= e < g[1]][0]
+            if e == lo:
+                y_banks[lo] = psum.tile([P, (hi - lo) * C], F32, name="y_ps", bufs=2)
+            y_ps = y_banks[lo]
+            nc.tensor.matmul_mx(
+                out=y_ps[:, (e - lo) * C : (e - lo + 1) * C],
+                lhsT=w2_q[e][0].bitcast(FP8X4),
+                lhsT_scale=w2_q[e][1],
+                rhs=h_q[e][0][:].bitcast(FP8X4),
+                rhs_scale=h_q[e][1][:],
+                start=True,
+                stop=True,
+            )
+            if e == hi - 1:
+                nc.scalar.copy(out=y_all[:, lo * C : hi * C], in_=y_ps[:])
+
+        def hidden_steps(e, b_ps, relu_a):
             held = {}
 
             def gate_hidden():
@@ -130,85 +158,109 @@ def tile_moe_ecr_glu_relu_kernel(
                 nc.vector.tensor_tensor(h_bf[:], b_ps[:].rearrange("p t c -> p c t"), relu_a[:], MULT)
                 held["h"] = h_bf
 
-            def multiply():
-                h_codes, h_scales = quantize(held["h"][:].rearrange("p c t -> p (c t)"), small, "h")
-                lo, hi = [g for g in Y_GROUPS if g[0] <= e < g[1]][0]
-                if e == lo:
-                    y_banks[lo] = psum.tile([P, (hi - lo) * C], F32, name="y_ps")
-                y_ps = y_banks[lo]
-                nc.tensor.matmul_mx(
-                    out=y_ps[:, (e - lo) * C : (e - lo + 1) * C],
-                    lhsT=w2_q[0][:].bitcast(FP8X4),
-                    lhsT_scale=w2_q[1][:],
-                    rhs=h_codes[:].bitcast(FP8X4),
-                    rhs_scale=h_scales[:],
-                    start=True,
-                    stop=True,
-                )
-                if e == hi - 1:
-                    nc.scalar.copy(out=y_all[:, lo * C : hi * C], in_=y_ps[:])
+            def quantize_hidden():
+                name = "half1_0" if e < E - 1 else "w2_bf"
+                codes = rounded.tile([P, C], U32, name=name, align_bytes=64)
+                h_q[e] = quantize(held["h"][:].rearrange("p c t -> p (c t)"), "h", codes)
+                if e in w2_q:
+                    second_layer(e)
 
-            return gate_hidden, multiply
+            return gate_hidden, quantize_hidden
+
+        def round_w2(raw):
+            w2_bf = rounded.tile([P, W2_GROUP, N, PACK], BF16, name="w2_bf", align_bytes=64)
+            for g in range(W2_GROUP):
+                nc.scalar.copy(
+                    out=w2_bf[:, g].rearrange("p (c i) j -> p c j i", i=4),
+                    in_=raw[:, g].rearrange("p j (c i) -> p c j i", i=4),
+                )
+            return w2_bf[:].rearrange("p g n j -> p (g n j)")
 
         tokens = None
-        behind = None
+        behind = (None, None)
         for e in range(E):
             cols = slice(e * C % GATHER, e * C % GATHER + C)
-            raw = first if e == 0 else load_rows(w1[e, 0:K_PASS, :])
-            w1_q = [quantize_first_layer(raw, 0, behind)]
-            w1_q.append(quantize_first_layer(load_rows(w1[e, K_PASS:K, :]), 1))
+            if 2 * e < WHOLE:
+                raws = first if e == 0 else load_blocks(w1[e])
+                halves = [round_pass(raws[:, o], o) for o in range(PASSES)]
+                w1_q = [quantize_pass(halves[o], behind[o]) for o in range(PASSES)]
+            else:
+                w1_q = [quantize_pass(round_pass(load_blocks(w1[e, 0:K_PASS, :])[:, 0], 0), behind[0])]
+                w1_q.append(quantize_pass(round_pass(load_blocks(w1[e, K_PASS:K, :])[:, 0], 1), behind[1]))
             if e * C % GATHER == 0:
                 tokens = gather_tokens(e * C // GATHER)
             a_ps = psum.tile([P, PACK, C], F32, name="a_ps")
             first_layer(a_ps, w1_q, tokens, cols)
 
-            w3_q = [quantize_first_layer(load_rows(w3[e, 0:K_PASS, :]), 2)]
-            relu_a = rounded.tile([P, C, PACK], F32, name="half2_0", align_bytes=64)
-            nc.scalar.activation(relu_a[:], a_ps[:].rearrange("p t c -> p c t"), RELU)
-            w3_q.append(quantize_first_layer(load_rows(w3[e, K_PASS:K, :]), 3))
+            def rectify(a_ps=a_ps):
+                relu_a = rounded.tile([P, C, PACK], F32, name="half2_0", align_bytes=64)
+                nc.scalar.activation(relu_a[:], a_ps[:].rearrange("p t c -> p c t"), RELU)
+                return relu_a
+
+            if 2 * e + 1 < WHOLE:
+                raws = load_blocks(w3[e])
+                halves = [round_pass(raws[:, o], PASSES + o) for o in range(PASSES)]
+                w3_q = [quantize_pass(halves[0])]
+                relu_a = rectify()
+                w3_q.append(quantize_pass(halves[1]))
+            else:
+                w3_q = [quantize_pass(round_pass(load_blocks(w3[e, 0:K_PASS, :])[:, 0], 2))]
+                relu_a = rectify()
+                extra = LAST_SHARE if e == E - 1 else 0
+                w3_q.append(quantize_pass(round_pass(load_blocks(w3[e, K_PASS:K, :])[:, 0], 3, extra)))
             b_ps = psum.tile([P, PACK, C], F32, name="b_ps")
             first_layer(b_ps, w3_q, tokens, cols)
+            behind = hidden_steps(e, b_ps, relu_a)
 
-            raw2 = load_rows(w2[e])
-            w2_bf = small.tile([P, N, PACK], BF16, name="w2_bf", align_bytes=64)
-            nc.scalar.copy(
-                out=w2_bf[:].rearrange("p (c i) j -> p c j i", i=4),
-                in_=raw2[:].rearrange("p j (c i) -> p c j i", i=4),
-            )
-            w2_q = quantize(w2_bf[:].rearrange("p n j -> p (n j)"), small, "w2")
-            behind = second_layer(e, b_ps, relu_a, w2_q)
-        for step in behind:
-            step()
+            if e in W2_AFTER:
+                lo = W2_GROUP * W2_AFTER.index(e)
+                w2_bf = round_w2(load_blocks(w2[lo : lo + W2_GROUP].rearrange("e i n -> (e i) n")))
+                if e == E - 1:
+                    behind[0]()
+                codes, scales = quantize(w2_bf, "w2")
+                for g in range(W2_GROUP):
+                    w2_q[lo + g] = (codes[:, g * N : (g + 1) * N], scales[:, g * N : (g + 1) * N])
+                    if lo + g in h_q:
+                        second_layer(lo + g)
+        behind[1]()
 
-        lists, gates = [], []
+        lists = []
         for r, pos in enumerate((pos1, pos2, pos3)):
             pos_sb = keep.tile([P, T // PER_COL], U16, name="pos%d" % r)
             nc.sync.dma_start(pos_sb[:], pos)
             lists.append(pos_sb)
-            gate_sb = stream.tile([P, T], F32, name="raw")
-            nc.sync.dma_start(out=gate_sb[:], in_=gate[r])
-            gates.append(gate_sb)
 
         t0 = 0
-        pending = None
         for i, width in enumerate(CHUNKS):
             cols = slice(t0, t0 + width)
+            on_tensor = i < ON_TENSOR
+            blocks = width // P
+            sums = [psum.tile([P, P], F32, name="sum_ps", bufs=4) for b in range(blocks)] if on_tensor else []
+            gates = stream.tile([P, TOP, width], F32, name="raw")
+            nc.sync.dma_start(out=gates[:], in_=gate[:, :, cols].rearrange("r p t -> p r t"))
             parts = []
             for r in range(TOP):
                 part = keep.tile([P, width], F32, name="part%d_%d" % (i, r))
                 idx = lists[r][:, t0 // PER_COL : (t0 + width) // PER_COL]
-                nc.vector.tensor_tensor(part[:], y_all[:].indirect(idx), gates[r][:, cols], MULT)
+                nc.vector.tensor_tensor(part[:], y_all[:].indirect(idx), gates[:, r, :], MULT)
                 parts.append(part)
-                if r == 0 and pending is not None:
-                    pending()
-            two = keep.tile([P, width], F32, name="two%d" % i)
-            nc.vector.tensor_tensor(two[:], parts[0][:], parts[1][:], ADD)
-
-            def finish(two=two, third=parts[2], cols=cols, width=width, i=i):
-                total = keep.tile([P, width], F32, name="total%d" % i)
-                nc.vector.tensor_tensor(total[:], two[:], third[:], ADD)
+                for b, acc in enumerate(sums):
+                    nc.tensor.matmul(
+                        acc[:], part[:, b * P : (b + 1) * P], ident[:],
+                        start=(r == 0), stop=(r == TOP - 1), is_transpose=True,
+                    )
+            total = keep.tile([P, width], F32, name="total%d" % i)
+            if on_tensor:
+                back = psum.tile([P, width], F32, name="a_ps" if i % 2 == 0 else "b_ps")
+                for b, acc in enumerate(sums):
+                    turned = keep.tile([P, P], F32, name="turned%d_%d" % (i, b))
+                    nc.scalar.copy(out=turned[:], in_=acc[:])
+                    nc.tensor.transpose(back[:, b * P : (b + 1) * P], turned[:], ident[:])
+                nc.scalar.copy(out=total[:], in_=back[:])
+                nc.scalar.dma_start(out=out[:, cols], in_=total[:])
+            else:
+                two = keep.tile([P, width], F32, name="two%d" % i)
+                nc.vector.tensor_tensor(two[:], parts[0][:], parts[1][:], ADD)
+                nc.vector.tensor_tensor(total[:], two[:], parts[2][:], ADD)
                 nc.sync.dma_start(out=out[:, cols], in_=total[:])
-
-            pending = finish
             t0 += width
-        pending()

@@ -29,9 +29,9 @@ GATHER = 256
 Y_GROUPS = ((0, 4), (4, 6), (6, 7), (7, 8))
 W2_GROUP = 2
 W2_AFTER = (0, 2, 4, 7)
-WHOLE = 2 * E - 3
+WHOLE = 2 * E - 2
 LAST_SHARE = 32
-CHUNKS = (256, 256, 256, 128, 128)
+CHUNKS = (256, 256, 256, 256)
 ON_TENSOR = 3
 
 
@@ -185,8 +185,8 @@ def tile_moe_ecr_glu_relu_kernel(
                 halves = [round_pass(raws[:, o], o) for o in range(PASSES)]
                 w1_q = [quantize_pass(halves[o], behind[o]) for o in range(PASSES)]
             else:
-                w1_q = [quantize_pass(round_pass(load_blocks(w1[e, 0:K_PASS, :])[:, 0], 0), behind[0])]
-                w1_q.append(quantize_pass(round_pass(load_blocks(w1[e, K_PASS:K, :])[:, 0], 1), behind[1]))
+                w1_q = [quantize_pass(round_pass(load_blocks(w1[e, 0:K_PASS, :])[:, 0], 0, LAST_SHARE), behind[0])]
+                w1_q.append(quantize_pass(round_pass(load_blocks(w1[e, K_PASS:K, :])[:, 0], 1, LAST_SHARE), behind[1]))
             if e * C % GATHER == 0:
                 tokens = gather_tokens(e * C // GATHER)
             a_ps = psum.tile([P, PACK, C], F32, name="a_ps")
@@ -204,9 +204,9 @@ def tile_moe_ecr_glu_relu_kernel(
                 relu_a = rectify()
                 w3_q.append(quantize_pass(halves[1]))
             else:
-                w3_q = [quantize_pass(round_pass(load_blocks(w3[e, 0:K_PASS, :])[:, 0], 2))]
+                w3_q = [quantize_pass(round_pass(load_blocks(w3[e, 0:K_PASS, :])[:, 0], 2, LAST_SHARE))]
                 relu_a = rectify()
-                extra = LAST_SHARE if e == E - 1 else 0
+                extra = LAST_SHARE
                 w3_q.append(quantize_pass(round_pass(load_blocks(w3[e, K_PASS:K, :])[:, 0], 3, extra)))
             b_ps = psum.tile([P, PACK, C], F32, name="b_ps")
             first_layer(b_ps, w3_q, tokens, cols)

from contextlib import ExitStack

import concourse.mybir as mybir
from concourse.masks import make_identity

K, T, E, C, H, N = 1024, 1024, 8, 128, 512, 128
TOP = 3
PAD = 64
FLOPS = 2 * E * C * (2 * K * H + H * N)

F32 = mybir.dt.float32
BF16 = mybir.dt.bfloat16
I32 = mybir.dt.int32
U32 = mybir.dt.uint32
U16 = mybir.dt.uint16
U8 = mybir.dt.uint8
FP8X4 = mybir.dt.float8_e4m3fn_x4
MULT = mybir.AluOpType.mult
ADD = mybir.AluOpType.add
RELU = mybir.ActivationFunctionType.Relu

P = 128
PACK = 4
K_PASS = P * PACK
PASSES = K // K_PASS
SLOTS = E * C
PER_COL = 16
GATHER = 256
Y_GROUPS = ((0, 4), (4, 6), (6, 7), (7, 8))
W2_GROUP = 2
W2_AFTER = (0, 2, 4, 7)
WHOLE = 2 * E - 2
LAST_SHARE = 32
CHUNKS = (256, 256, 256, 256)
ON_TENSOR = 3


def tile_moe_ecr_glu_relu_kernel(
    tc, x_words, x_scales, w1, w3, w2, gate, offs, pos1, pos2, pos3, out
):
    nc = tc.nc
    with ExitStack() as ctx:
        keep = ctx.enter_context(tc.tile_pool(name="keep", bufs=1))
        stream = ctx.enter_context(tc.tile_pool(name="stream", bufs=8))
        rounded = ctx.enter_context(tc.tile_pool(name="rounded", bufs=1))
        coded = ctx.enter_context(tc.tile_pool(name="coded", bufs=4))
        small = ctx.enter_context(tc.tile_pool(name="small", bufs=4))
        psum = ctx.enter_context(tc.psum_pool(name="psum", bufs=1))

        def load_blocks(rows):
            blocks = rows.shape[0] // K_PASS
            raw = stream.tile([P, blocks, PACK, rows.shape[1]], F32, name="raw")
            nc.sync.dma_start(out=raw[:], in_=rows.rearrange("(g p j) c -> p g j c", p=P, j=PACK))
            return raw

        def quantize(values, name, codes=None):
            width = values.shape[1] // PACK
            if codes is None:
                codes = small.tile([P, width], U32, name=name + "_codes", align_bytes=64)
            scales = small.tile([P, width], U8, name=name + "_scales", align_bytes=64)
            nc.vector.quantize_mx(out=codes[:].bitcast(FP8X4), scales=scales[:], in_=values)
            return codes, scales

        def round_pass(raw, place, vector_extra=0):
            src = raw.rearrange("p j (m t) -> p m j t", t=PACK)
            halves, views = [], []
            for u in range(2):
                half = rounded.tile([P, 2 * H], BF16, name="half%d_%d" % (place, u), align_bytes=64)
                halves.append(half)
                views.append(half[:].rearrange("p (t m j) -> p m j t", t=2, j=PACK))
            nc.vector.tensor_copy(out=views[0], in_=src[:, :, :, 0:2])
            if vector_extra:
                nc.vector.tensor_copy(out=views[1][:, 0:vector_extra], in_=src[:, 0:vector_extra, :, 2:4])
            nc.scalar.copy(out=views[1][:, vector_extra:P], in_=src[:, vector_extra:P, :, 2:4])
            return halves

        def quantize_pass(halves, between=None):
            codes = coded.tile([P, H], U32, name="w_codes", align_bytes=64)
            scales = coded.tile([P, H], U8, name="w_scales", align_bytes=64)
            for u in range(2):
                cols = slice(u * H // 2, (u + 1) * H // 2)
                nc.vector.quantize_mx(out=codes[:, cols].bitcast(FP8X4), scales=scales[:, cols], in_=halves[u][:])
                if between is not None and u == 0:
                    between()
            return codes, scales

        first = load_blocks(w1[0])

        offs_sb = keep.tile([P, SLOTS // PER_COL], U16, name="offs_sb")
        nc.sync.dma_start(offs_sb[:], offs)
        xs = keep.tile([P, T], U8, name="xs", align_bytes=64)
        nc.vector.memset(xs[:].bitcast(I32), 0)
        for q in range(4):
            nc.scalar.dma_start(
                out=xs[32 * q : 32 * q + 4 * PASSES, :].bitcast(I32),
                in_=x_scales[:, 4 * q : 4 * q + 4, :].bitcast(I32),
            )
        xw = keep.tile([P, PASSES, T], I32, name="xw", align_bytes=64)
        nc.sync.dma_start(out=xw[:], in_=x_words.rearrange("o p t r -> p o (t r)").bitcast(I32))

        y_all = keep.tile([P, SLOTS + PAD], F32, name="y_all")
        nc.vector.memset(y_all[:, SLOTS:], 0.0)
        ident = keep.tile([P, P], F32, name="ident")
        make_identity(nc, ident[:])

        def gather_tokens(g):
            idx = offs_sb[:, g * GATHER // PER_COL : (g + 1) * GATHER // PER_COL]
            words = []
            for o in range(PASSES):
                gw = keep.tile([P, GATHER], U32, name="gw%d_%d" % (g, o), align_bytes=64)
                nc.vector.tensor_copy(gw[:], xw[:, o, :].bitcast(U32).indirect(idx))
                words.append(gw)
            gs = keep.tile([P, GATHER], U8, name="gs%d" % g, align_bytes=64)
            nc.vector.tensor_copy(gs[:], xs[:].indirect(idx))
            return words, gs

        def first_layer(acc, passes, tokens, cols):
            words, gs = tokens
            for t in range(PACK):
                mcols = slice(t * P, (t + 1) * P)
                for o in range(PASSES):
                    codes, scales = passes[o]
                    nc.tensor.matmul_mx(
                        out=acc[:, t, :],
                        lhsT=codes[:, mcols].bitcast(FP8X4),
                        lhsT_scale=scales[:, mcols],
                        rhs=words[o][:, cols].bitcast(FP8X4),
                        rhs_scale=gs[4 * o : P, cols],
                        start=(o == 0),
                        stop=(o == PASSES - 1),
                    )

        y_banks, w2_q, h_q = {}, {}, {}

        def second_layer(e):
            lo, hi = [g for g in Y_GROUPS if g[0] <= e < g[1]][0]
            if e == lo:
                y_banks[lo] = psum.tile([P, (hi - lo) * C], F32, name="y_ps", bufs=2)
            y_ps = y_banks[lo]
            nc.tensor.matmul_mx(
                out=y_ps[:, (e - lo) * C : (e - lo + 1) * C],
                lhsT=w2_q[e][0].bitcast(FP8X4),
                lhsT_scale=w2_q[e][1],
                rhs=h_q[e][0][:].bitcast(FP8X4),
                rhs_scale=h_q[e][1][:],
                start=True,
                stop=True,
            )
            if e == hi - 1:
                nc.scalar.copy(out=y_all[:, lo * C : hi * C], in_=y_ps[:])

        def hidden_steps(e, b_ps, relu_a):
            held = {}

            def gate_hidden():
                name = "half0_0" if e < E - 1 else "h_last"
                h_bf = rounded.tile([P, C, PACK], BF16, name=name, align_bytes=64)
                nc.vector.tensor_tensor(h_bf[:], b_ps[:].rearrange("p t c -> p c t"), relu_a[:], MULT)
                held["h"] = h_bf

            def quantize_hidden():
                name = "half1_0" if e < E - 1 else "w2_bf"
                codes = rounded.tile([P, C], U32, name=name, align_bytes=64)
                h_q[e] = quantize(held["h"][:].rearrange("p c t -> p (c t)"), "h", codes)
                if e in w2_q:
                    second_layer(e)

            return gate_hidden, quantize_hidden

        def round_w2(raw):
            w2_bf = rounded.tile([P, W2_GROUP, N, PACK], BF16, name="w2_bf", align_bytes=64)
            for g in range(W2_GROUP):
                nc.scalar.copy(
                    out=w2_bf[:, g].rearrange("p (c i) j -> p c j i", i=4),
                    in_=raw[:, g].rearrange("p j (c i) -> p c j i", i=4),
                )
            return w2_bf[:].rearrange("p g n j -> p (g n j)")

        tokens = None
        behind = (None, None)
        for e in range(E):
            cols = slice(e * C % GATHER, e * C % GATHER + C)
            if 2 * e < WHOLE:
                raws = first if e == 0 else load_blocks(w1[e])
                halves = [round_pass(raws[:, o], o) for o in range(PASSES)]
                w1_q = [quantize_pass(halves[o], behind[o]) for o in range(PASSES)]
            else:
                w1_q = [quantize_pass(round_pass(load_blocks(w1[e, 0:K_PASS, :])[:, 0], 0, LAST_SHARE), behind[0])]
                w1_q.append(quantize_pass(round_pass(load_blocks(w1[e, K_PASS:K, :])[:, 0], 1, LAST_SHARE), behind[1]))
            if e * C % GATHER == 0:
                tokens = gather_tokens(e * C // GATHER)
            a_ps = psum.tile([P, PACK, C], F32, name="a_ps")
            first_layer(a_ps, w1_q, tokens, cols)

            def rectify(a_ps=a_ps):
                relu_a = rounded.tile([P, C, PACK], F32, name="half2_0", align_bytes=64)
                nc.scalar.activation(relu_a[:], a_ps[:].rearrange("p t c -> p c t"), RELU)
                return relu_a

            if 2 * e + 1 < WHOLE:
                raws = load_blocks(w3[e])
                halves = [round_pass(raws[:, o], PASSES + o) for o in range(PASSES)]
                w3_q = [quantize_pass(halves[0])]
                relu_a = rectify()
                w3_q.append(quantize_pass(halves[1]))
            else:
                w3_q = [quantize_pass(round_pass(load_blocks(w3[e, 0:K_PASS, :])[:, 0], 2, LAST_SHARE))]
                relu_a = rectify()
                extra = LAST_SHARE
                w3_q.append(quantize_pass(round_pass(load_blocks(w3[e, K_PASS:K, :])[:, 0], 3, extra)))
            b_ps = psum.tile([P, PACK, C], F32, name="b_ps")
            first_layer(b_ps, w3_q, tokens, cols)
            behind = hidden_steps(e, b_ps, relu_a)

            if e in W2_AFTER:
                lo = W2_GROUP * W2_AFTER.index(e)
                w2_bf = round_w2(load_blocks(w2[lo : lo + W2_GROUP].rearrange("e i n -> (e i) n")))
                if e == E - 1:
                    behind[0]()
                codes, scales = quantize(w2_bf, "w2")
                for g in range(W2_GROUP):
                    w2_q[lo + g] = (codes[:, g * N : (g + 1) * N], scales[:, g * N : (g + 1) * N])
                    if lo + g in h_q:
                        second_layer(lo + g)
        behind[1]()

        lists = []
        for r, pos in enumerate((pos1, pos2, pos3)):
            pos_sb = keep.tile([P, T // PER_COL], U16, name="pos%d" % r)
            nc.sync.dma_start(pos_sb[:], pos)
            lists.append(pos_sb)

        t0 = 0
        for i, width in enumerate(CHUNKS):
            cols = slice(t0, t0 + width)
            on_tensor = i < ON_TENSOR
            blocks = width // P
            sums = [psum.tile([P, P], F32, name="sum_ps", bufs=4) for b in range(blocks)] if on_tensor else []
            gates = stream.tile([P, TOP, width], F32, name="raw")
            nc.sync.dma_start(out=gates[:], in_=gate[:, :, cols].rearrange("r p t -> p r t"))
            parts = []
            for r in range(TOP):
                part = keep.tile([P, width], F32, name="part%d_%d" % (i, r))
                idx = lists[r][:, t0 // PER_COL : (t0 + width) // PER_COL]
                nc.vector.tensor_tensor(part[:], y_all[:].indirect(idx), gates[:, r, :], MULT)
                parts.append(part)
                for b, acc in enumerate(sums):
                    nc.tensor.matmul(
                        acc[:], part[:, b * P : (b + 1) * P], ident[:],
                        start=(r == 0), stop=(r == TOP - 1), is_transpose=True,
                    )
            total = keep.tile([P, width], F32, name="total%d" % i)
            if on_tensor:
                back = psum.tile([P, width], F32, name="a_ps" if i % 2 == 0 else "b_ps")
                for b, acc in enumerate(sums):
                    turned = keep.tile([P, P], F32, name="turned%d_%d" % (i, b))
                    nc.scalar.copy(out=turned[:], in_=acc[:])
                    nc.tensor.transpose(back[:, b * P : (b + 1) * P], turned[:], ident[:])
                nc.scalar.copy(out=total[:], in_=back[:])
                nc.scalar.dma_start(out=out[:, cols], in_=total[:])
            else:
                two = keep.tile([P, width], F32, name="two%d" % i)
                nc.vector.tensor_tensor(two[:], parts[0][:], parts[1][:], ADD)
                nc.vector.tensor_tensor(total[:], two[:], parts[2][:], ADD)
                nc.sync.dma_start(out=out[:, cols], in_=total[:])
            t0 += width
